import numpy as np
import ml_dtypes


def mxq(x, axis, fmt="e4m3"):
    dtype, down = {"e4m3": (ml_dtypes.float8_e4m3fn, 7), "e5m2": (ml_dtypes.float8_e5m2, 14)}[fmt]
    v = np.moveaxis(np.asarray(x, np.float32).astype(ml_dtypes.bfloat16).astype(np.float64), axis, -1)
    blocks = v.reshape(v.shape[:-1] + (-1, 32))
    amax = np.abs(blocks).max(-1, keepdims=True)
    byte = np.maximum(np.where(amax > 0, np.frexp(amax)[1] - 1 + 127, 0) - down, 1)
    scale = np.exp2(byte - 127.0)
    codes = (blocks / scale).astype(np.float32).astype(dtype).astype(np.float64)
    return np.moveaxis((codes * scale).reshape(v.shape), -1, axis)


WIDE = False


def mx_kscale(k):
    if not WIDE:
        return np.ones(k)
    levels = np.array([10, -10, 5, -5, 0])
    if k % 512:
        return np.exp2(np.random.permutation(np.resize(levels, k // 32))).repeat(32)
    a = np.empty((k // 512, 16))
    for p in range(k // 512):
        a[p, :8] = np.random.permutation(np.resize(levels, 8))
        for g in range(8):
            far = levels[np.abs(levels - a[p, g]) >= 10]
            a[p, g + 8] = far[np.random.randint(len(far))]
    return np.exp2(a.ravel()).repeat(32)


def f64(x):
    return np.asarray(x).astype(np.float64)


def striped(idx):
    return np.tile(idx.reshape(-1, 16).T, (8, 1)).astype(np.uint16)


def unstriped(offs):
    return offs[:16].T.reshape(-1).astype(np.int64)


def striped8(idx):
    return np.concatenate([x.reshape(-1, 16).T for x in idx]).astype(np.uint16)


def runs(offs, k):
    lists = np.stack([offs[16 * r : 16 * r + 16].T.reshape(-1) for r in range(8)]).astype(np.int64)
    return lists[np.arange(k) % 512 // 64]


def pack_weight(w):
    k, n = w.shape
    w = f64(np.asarray(w, np.float32).astype(ml_dtypes.bfloat16)).reshape(k // 32, 32, n)
    amax = np.abs(w).max(1)
    byte = np.clip(np.where(amax > 0, np.frexp(amax)[1] - 1 + 127 - 7, 1), 1, 254)
    scaled = (w * np.exp2(127.0 - byte)[:, None, :]).reshape(k, n).astype(np.float32)
    words = np.ascontiguousarray(scaled.reshape(k // 512, 128, 4, n).transpose(0, 1, 3, 2)).astype(ml_dtypes.float8_e4m3fn).view(np.uint8)
    return words, np.ascontiguousarray(byte.astype(np.uint8).reshape(k // 512, 16, n))


def unpack_weight(words, scales):
    g, p, n, _ = words.shape
    vals = np.ascontiguousarray(words).view(ml_dtypes.float8_e4m3fn).astype(np.float64) * np.repeat(np.exp2(scales.astype(np.float64) - 127.0), 8, axis=1)[..., None]
    return vals.transpose(0, 1, 3, 2).reshape(g * 512, n)


K, T, S, G, H = 512, 1024, 512, 2048, 512


def setup_inputs():
    n = np.random.standard_normal
    s = mx_kscale(K)[:, None]
    packed_xT = pack_weight(n((K, T)) * s)
    packed_dT = pack_weight(n((K, G)) / s)
    return {
        "x_words": packed_xT[0],
        "x_scales": packed_xT[1],
        "d_words": packed_dT[0],
        "d_scales": packed_dT[1],
        "gs": (np.random.uniform(0.5, 1.5, (K, 1)) * s).astype(np.float32),
        "offs": striped(np.random.permutation(T)[:S]),
        "k1": striped8(np.random.randint(0, G, (8, H))),
        "n1": striped8(np.stack([np.random.permutation(S) for _ in range(8)])),
        "n2": striped8(np.stack([np.random.permutation(S) for _ in range(8)])),
        "k2": striped8(np.random.randint(0, G, (8, H))),
        "n3": striped8(np.stack([np.random.permutation(S) for _ in range(8)])),
        "n4": striped8(np.stack([np.random.permutation(S) for _ in range(8)])),
        "n5": striped8(np.stack([np.random.permutation(S) for _ in range(8)])),
    }


def reference(x_words, x_scales, d_words, d_scales, gs, offs, k1, n1, n2, k2, n3, n4, n5):
    d_k2 = unpack_weight(d_words, d_scales)[np.arange(K)[:, None], runs(k2, K)]
    d_k1 = unpack_weight(d_words, d_scales)[np.arange(K)[:, None], runs(k1, K)]
    xq = unpack_weight(x_words, x_scales)[:, unstriped(offs)]
    h = 0.0625 * (d_k1.T @ xq)
    z = f64(gs) * (np.maximum(h[np.arange(H)[:, None], runs(n1, H)], h[np.arange(H)[:, None], runs(n2, H)]) - (0.75 * h))
    h2 = 0.0625 * ((d_k2.T @ mxq(z, 0, "e4m3")))
    ex = np.exp(0.5 * h2)
    return np.log((ex + ex[np.arange(H)[:, None], runs(n3, H)]) / (ex[np.arange(H)[:, None], runs(n4, H)] + ex[np.arange(H)[:, None], runs(n5, H)]))

@@ -1,0 +1,185 @@
+from contextlib import ExitStack
+
+import concourse.mybir as mybir
+
+F32 = mybir.dt.float32
+BF16 = mybir.dt.bfloat16
+I32 = mybir.dt.int32
+U32 = mybir.dt.uint32
+U16 = mybir.dt.uint16
+U8 = mybir.dt.uint8
+FP8X4 = mybir.dt.float8_e4m3fn_x4
+ALU = mybir.AluOpType
+ACT = mybir.ActivationFunctionType
+
+P = 128
+T, G, S = 1024, 2048, 512
+HALF = S // 2
+HCOLS = HALF // 16
+FLOPS = 2 * 2 * 512 * 512 * 512
+
+
+def tile_picked_codeoverodds_none_p_kernel(
+    tc, x_words, x_scales, d_words, d_scales, gs, offs, k1, n1, n2, k2, n3, n4, n5, out
+):
+    nc = tc.nc
+    with ExitStack() as ctx:
+        lists = ctx.enter_context(tc.tile_pool(name="lists", bufs=1))
+        keep = ctx.enter_context(tc.tile_pool(name="keep", bufs=1))
+        ring = ctx.enter_context(tc.tile_pool(name="ring", bufs=3))
+        psum = ctx.enter_context(tc.psum_pool(name="psum", bufs=1))
+
+        def load_list(name, src):
+            tile = lists.tile([P, S // 16], U16, name=name)
+            nc.sync.dma_start(tile[:], src)
+            return tile
+
+        d_bytes = keep.tile([P, G], U8, name="d_bytes")
+        x_bytes = keep.tile([P, T], U8, name="x_bytes")
+        plane1 = keep.tile([P, 2 * S], U8, name="plane1", align_bytes=64)
+        plane2 = keep.tile([P, S], U8, name="plane2", align_bytes=64)
+        nc.vector.memset(plane1[:].bitcast(I32), 0)
+        nc.vector.memset(plane2[:].bitcast(I32), 0)
+
+        k1_l = load_list("k1_l", k1)
+        nc.sync.dma_start(d_bytes[:].bitcast(I32), d_scales[0].bitcast(I32).unsqueeze(1).to_broadcast([16, 8, G // 4]))
+        offs_l = load_list("offs_l", offs)
+        nc.sync.dma_start(x_bytes[:].bitcast(I32), x_scales[0].bitcast(I32).unsqueeze(1).to_broadcast([16, 8, T // 4]))
+        x_tab = keep.tile([P, T], I32, name="x_tab")
+        d_tab = keep.tile([P, G], I32, name="d_tab")
+        nc.sync.dma_start(x_tab[:], x_words[0].rearrange("p n t -> p (n t)").bitcast(I32))
+        g_raw = keep.tile([P, 4], F32, name="g_raw")
+        nc.gpsimd.dma_start(g_raw[:], gs.rearrange("(p t) o -> p (t o)", t=4))
+        n1_l = load_list("n1_l", n1)
+        n2_l = load_list("n2_l", n2)
+        k2_l = load_list("k2_l", k2)
+        nc.sync.dma_start(d_tab[:], d_words[0].rearrange("p n t -> p (n t)").bitcast(I32))
+        n4_l = load_list("n4_l", n4)
+        n5_l = load_list("n5_l", n5)
+        n3_l = load_list("n3_l", n3)
+
+        gain = keep.tile([P, 4], F32, name="gain")
+        nc.scalar.activation(gain[:], g_raw[:], ACT.Copy, scale=0.0625)
+
+        def place_rows(plane, picked, queues):
+            for j in range(4):
+                queues[j % len(queues)].dma_start(
+                    plane[:].bitcast(I32)[j:P:32, :], picked[:].bitcast(I32)[8 * j : P : 32, :]
+                )
+
+        def deal(dst, src):
+            nc.vector.tensor_copy(
+                dst.rearrange("p (t m) -> p t m", t=4), src.rearrange("p (m t) -> p t m", t=4)
+            )
+
+        picked1 = keep.tile([P, 2 * S], U8, name="picked1")
+        nc.vector.tensor_copy(picked1[:, S:], d_bytes[:].indirect(k1_l[:]))
+        nc.vector.tensor_copy(picked1[:, :S], x_bytes[:].indirect(offs_l[:]))
+        place_rows(plane1, picked1, (nc.scalar,))
+        x_codes = keep.tile([P, S], U32, name="x_codes", align_bytes=64)
+        nc.vector.tensor_copy(x_codes[:], x_tab[:].bitcast(U32).indirect(offs_l[:]))
+        picked_w1 = keep.tile([P, S], U32, name="picked_w1", tag="picked")
+        nc.vector.tensor_copy(picked_w1[:], d_tab[:].bitcast(U32).indirect(k1_l[:]))
+        w1_codes = keep.tile([P, S], U32, name="w1_codes", align_bytes=64)
+        w1_scales = keep.tile([P, S], U8, name="w1_scales", align_bytes=64)
+        deal(w1_scales[:], plane1[:, S:])
+        deal(w1_codes[:], picked_w1[:])
+
+        acc1 = [psum.tile([P, S], F32, name=f"acc1_{t}", tag=f"low{t}") for t in range(4)]
+        for t in range(4):
+            cols = slice(t * P, (t + 1) * P)
+            nc.tensor.matmul_mx(
+                out=acc1[t][:], lhsT=w1_codes[:, cols].bitcast(FP8X4), lhsT_scale=w1_scales[:, cols],
+                rhs=x_codes[:].bitcast(FP8X4), rhs_scale=plane1[:, :S], start=True, stop=True,
+            )
+
+        picked2 = keep.tile([P, S], U8, name="picked2", tag="picked")
+        nc.vector.tensor_copy(picked2[:], d_bytes[:].indirect(k2_l[:]))
+        place_rows(plane2, picked2, (nc.sync,))
+        picked_w2 = keep.tile([P, S], U32, name="picked_w2", tag="picked")
+        nc.vector.tensor_copy(picked_w2[:], d_tab[:].bitcast(U32).indirect(k2_l[:]))
+        w2_codes = keep.tile([P, S], U32, name="w2_codes", align_bytes=64)
+        w2_scales = keep.tile([P, S], U8, name="w2_scales", align_bytes=64)
+        deal(w2_codes[:], picked_w2[:])
+        deal(w2_scales[:], plane2[:])
+
+        halves = [slice(0, HALF), slice(HALF, S)]
+        lhalves = [slice(0, HCOLS), slice(HCOLS, 2 * HCOLS)]
+        h = [keep.tile([P, S], F32, name=f"h{t}") for t in range(4)]
+        own = [[keep.tile([P, HALF], F32, name=f"own{t}_{c}") for c in range(2)] for t in range(4)]
+        for t in range(4):
+            nc.scalar.copy(h[t][:], acc1[t][:])
+            nc.scalar.activation(own[t][0][:], acc1[t][:, halves[0]], ACT.Copy, scale=0.75)
+        for t in range(4):
+            nc.scalar.activation(own[t][1][:], acc1[t][:, halves[1]], ACT.Copy, scale=0.75)
+
+        ex = [keep.tile([P, S], F32, name=f"ex{t}") for t in range(4)]
+        ex_own = [[keep.tile([P, HALF], F32, name=f"exown{t}_{c}") for c in range(2)] for t in range(4)]
+        arg = [None] + [keep.tile([P, S], F32, name=f"arg{t}", tag=f"arg{t}") for t in range(1, 4)]
+        for c in range(2):
+            z_rows = keep.tile([P, 4, HALF], BF16, name=f"z_rows{c}")
+            for t in range(4):
+                u = ring.tile([P, HALF], F32, name="u")
+                v = ring.tile([P, HALF], F32, name="v")
+                m = ring.tile([P, HALF], F32, name="m")
+                nc.vector.tensor_tensor(u[:], h[t][:].indirect(n1_l[:, lhalves[c]]), own[t][c][:], ALU.subtract)
+                nc.vector.tensor_tensor(v[:], h[t][:].indirect(n2_l[:, lhalves[c]]), own[t][c][:], ALU.subtract)
+                nc.vector.tensor_tensor(m[:], u[:], v[:], ALU.max)
+                nc.scalar.activation(z_rows[:, t, :], m[:], ACT.Copy, scale=gain[:, t : t + 1])
+            z_packed = keep.tile([P, HALF, 4], BF16, name=f"z_packed{c}", align_bytes=64)
+            weave = nc.scalar.copy if c == 0 else nc.vector.tensor_copy
+            weave(z_packed[:], z_rows[:].rearrange("p t j -> p j t"))
+            z_codes = keep.tile([P, HALF], U32, name=f"z_codes{c}", align_bytes=64)
+            z_scales = keep.tile([P, HALF], U8, name=f"z_scales{c}", align_bytes=64)
+            nc.vector.quantize_mx(
+                out=z_codes[:].bitcast(FP8X4), scales=z_scales[:], in_=z_packed[:].rearrange("p j t -> p (j t)")
+            )
+            for t in range(4):
+                cols = slice(t * P, (t + 1) * P)
+                acc2 = psum.tile([P, HALF], F32, name=f"acc2_{t}_{c}", tag=f"high{t}" if c == 0 else f"low{t}")
+                nc.tensor.matmul_mx(
+                    out=acc2[:], lhsT=w2_codes[:, cols].bitcast(FP8X4), lhsT_scale=w2_scales[:, cols],
+                    rhs=z_codes[:].bitcast(FP8X4), rhs_scale=z_scales[:], start=True, stop=True,
+                )
+                nc.scalar.activation(ex[t][:, halves[c]], acc2[:], ACT.Exp, scale=0.03125)
+                nc.sync.dma_start(ex_own[t][c][:], ex[t][:, halves[c]])
+                if t > 0:
+                    nc.scalar.activation(arg[t][:, halves[c]], acc2[:], ACT.Copy, scale=0.03125)
+
+        e4 = [[keep.tile([P, HALF], F32, name=f"e4_{t}_{c}") for c in range(2)] for t in range(4)]
+        for t in range(1, 4):
+            for c in range(2):
+                nc.scalar.activation(e4[t][c][:], arg[t][:].indirect(n4_l[:, lhalves[c]]), ACT.Exp)
+        for c in range(2):
+            nc.vector.tensor_copy(e4[0][c][:], ex[0][:].indirect(n4_l[:, lhalves[c]]))
+
+        sums = [keep.tile([P, 2, S], F32, name=f"sums{t}") for t in range(4)]
+
+        def numer(t, c):
+            nc.vector.tensor_tensor(sums[t][:, 0, halves[c]], ex[t][:].indirect(n3_l[:, lhalves[c]]), ex_own[t][c][:], ALU.add)
+
+        def denom(t, c):
+            nc.vector.tensor_tensor(sums[t][:, 1, halves[c]], ex[t][:].indirect(n5_l[:, lhalves[c]]), e4[t][c][:], ALU.add)
+
+        numer(0, 0)
+        denom(0, 0)
+        denom(0, 1)
+        numer(0, 1)
+        for t in range(1, 4):
+            for c in range(2):
+                numer(t, c)
+            for c in range(2):
+                denom(t, c)
+
+        logs = keep.tile([P, 4, 2, S], F32, name="logs", tag="arg3")
+        rows = out.rearrange("(p t) j -> t p j", t=4)
+        res = [keep.tile([P, S], F32, name=f"res{t}") for t in range(4)]
+        for t in range(3):
+            nc.scalar.activation(logs[:, t], sums[t][:], ACT.Ln)
+            nc.vector.tensor_tensor(res[t][:], logs[:, t, 0, :], logs[:, t, 1, :], ALU.subtract)
+            nc.sync.dma_start(rows[t], res[t][:])
+        nc.scalar.activation(logs[:, 3, 0, :], sums[3][:, 0, :], ACT.Ln)
+        for c in range(2):
+            nc.scalar.activation(logs[:, 3, 1, halves[c]], sums[3][:, 1, halves[c]], ACT.Ln)
+            nc.vector.tensor_tensor(res[3][:, halves[c]], logs[:, 3, 0, halves[c]], logs[:, 3, 1, halves[c]], ALU.subtract)
+            nc.sync.dma_start(rows[3][:, halves[c]], res[3][:, halves[c]])

@@ -16,6 +16,7 @@ P = 128
 T, G, S = 1024, 2048, 512
 HALF = S // 2
 HCOLS = HALF // 16
+SCALAR_TILES = (1, 2, 3)
 FLOPS = 2 * 2 * 512 * 512 * 512
 
 
@@ -26,7 +27,6 @@ def tile_picked_codeoverodds_none_p_kernel(
     with ExitStack() as ctx:
         lists = ctx.enter_context(tc.tile_pool(name="lists", bufs=1))
         keep = ctx.enter_context(tc.tile_pool(name="keep", bufs=1))
-        ring = ctx.enter_context(tc.tile_pool(name="ring", bufs=3))
         psum = ctx.enter_context(tc.psum_pool(name="psum", bufs=1))
 
         def load_list(name, src):
@@ -36,72 +36,79 @@ def tile_picked_codeoverodds_none_p_kernel(
 
         d_bytes = keep.tile([P, G], U8, name="d_bytes")
         x_bytes = keep.tile([P, T], U8, name="x_bytes")
-        plane1 = keep.tile([P, 2 * S], U8, name="plane1", align_bytes=64)
-        plane2 = keep.tile([P, S], U8, name="plane2", align_bytes=64)
-        nc.vector.memset(plane1[:].bitcast(I32), 0)
-        nc.vector.memset(plane2[:].bitcast(I32), 0)
-
-        k1_l = load_list("k1_l", k1)
-        nc.sync.dma_start(d_bytes[:].bitcast(I32), d_scales[0].bitcast(I32).unsqueeze(1).to_broadcast([16, 8, G // 4]))
-        offs_l = load_list("offs_l", offs)
-        nc.sync.dma_start(x_bytes[:].bitcast(I32), x_scales[0].bitcast(I32).unsqueeze(1).to_broadcast([16, 8, T // 4]))
         x_tab = keep.tile([P, T], I32, name="x_tab")
         d_tab = keep.tile([P, G], I32, name="d_tab")
-        nc.sync.dma_start(x_tab[:], x_words[0].rearrange("p n t -> p (n t)").bitcast(I32))
         g_raw = keep.tile([P, 4], F32, name="g_raw")
-        nc.gpsimd.dma_start(g_raw[:], gs.rearrange("(p t) o -> p (t o)", t=4))
+
+        offs_l = load_list("offs_l", offs)
+        nc.sync.dma_start(x_bytes[:].bitcast(I32), x_scales[0].bitcast(I32).unsqueeze(1).to_broadcast([16, 8, T // 4]))
+        k1_l = load_list("k1_l", k1)
+        nc.sync.dma_start(d_bytes[:].bitcast(I32), d_scales[0].bitcast(I32).unsqueeze(1).to_broadcast([16, 8, G // 4]))
+        k2_l = load_list("k2_l", k2)
+        nc.sync.dma_start(x_tab[:], x_words[0].rearrange("p n t -> p (n t)").bitcast(I32))
         n1_l = load_list("n1_l", n1)
         n2_l = load_list("n2_l", n2)
-        k2_l = load_list("k2_l", k2)
+        nc.sync.dma_start(g_raw[:], gs.rearrange("(p t) o -> p (t o)", t=4))
         nc.sync.dma_start(d_tab[:], d_words[0].rearrange("p n t -> p (n t)").bitcast(I32))
         n4_l = load_list("n4_l", n4)
         n5_l = load_list("n5_l", n5)
         n3_l = load_list("n3_l", n3)
 
+        plane1 = keep.tile([P, 2 * S], U8, name="plane1", tag="plane1")
+        plane2 = keep.tile([P, S], U8, name="plane2")
+        nc.vector.memset(plane1[:].bitcast(I32), 0)
+        nc.vector.memset(plane2[:].bitcast(I32), 0)
+        first_scale = keep.tile([P, 1], F32, name="first_scale", tag="z_pairs1")
+        nc.vector.memset(first_scale[:], 0.03125)
+        ex = [keep.tile([P, 2 * S], F32, name=f"ex{t}") for t in range(4)]
+        arg = {t: keep.tile([P, 2 * S], F32, name=f"arg{t}", tag=f"arg{t}") for t in SCALAR_TILES}
+        for window in ex + list(arg.values()):
+            nc.gpsimd.memset(window[:, S:], 0.0)
+
         gain = keep.tile([P, 4], F32, name="gain")
         nc.scalar.activation(gain[:], g_raw[:], ACT.Copy, scale=0.0625)
 
-        def place_rows(plane, picked, queues):
+        def place_rows(plane, picked):
             for j in range(4):
-                queues[j % len(queues)].dma_start(
-                    plane[:].bitcast(I32)[j:P:32, :], picked[:].bitcast(I32)[8 * j : P : 32, :]
-                )
+                nc.sync.dma_start(plane[:].bitcast(I32)[j:P:32, :], picked[:].bitcast(I32)[8 * j : P : 32, :])
 
-        def deal(dst, src):
+        def deal(dst, src, run):
             nc.vector.tensor_copy(
-                dst.rearrange("p (t m) -> p t m", t=4), src.rearrange("p (m t) -> p t m", t=4)
+                dst.rearrange("p (t a r) -> p t a r", t=4, r=run), src.rearrange("p (a t r) -> p t a r", t=4, r=run)
             )
 
         picked1 = keep.tile([P, 2 * S], U8, name="picked1")
-        nc.vector.tensor_copy(picked1[:, S:], d_bytes[:].indirect(k1_l[:]))
         nc.vector.tensor_copy(picked1[:, :S], x_bytes[:].indirect(offs_l[:]))
-        place_rows(plane1, picked1, (nc.scalar,))
+        nc.vector.tensor_copy(picked1[:, S:], d_bytes[:].indirect(k1_l[:]))
+        place_rows(plane1, picked1)
+        picked2 = keep.tile([P, S], U8, name="picked2")
+        nc.vector.tensor_copy(picked2[:], d_bytes[:].indirect(k2_l[:]))
+        place_rows(plane2, picked2)
         x_codes = keep.tile([P, S], U32, name="x_codes", align_bytes=64)
         nc.vector.tensor_copy(x_codes[:], x_tab[:].bitcast(U32).indirect(offs_l[:]))
-        picked_w1 = keep.tile([P, S], U32, name="picked_w1", tag="picked")
+        picked_w1 = keep.tile([P, S], U32, name="picked_w1")
         nc.vector.tensor_copy(picked_w1[:], d_tab[:].bitcast(U32).indirect(k1_l[:]))
         w1_codes = keep.tile([P, S], U32, name="w1_codes", align_bytes=64)
         w1_scales = keep.tile([P, S], U8, name="w1_scales", align_bytes=64)
-        deal(w1_scales[:], plane1[:, S:])
-        deal(w1_codes[:], picked_w1[:])
+        deal(w1_codes[:], picked_w1[:], 1)
+        x_plane = keep.tile([P, S], U8, name="x_plane", align_bytes=64)
+        nc.vector.tensor_copy(x_plane[:].bitcast(I32), plane1[:, :S].bitcast(I32))
+        deal(w1_scales[:], plane1[:, S:], 1)
 
         acc1 = [psum.tile([P, S], F32, name=f"acc1_{t}", tag=f"low{t}") for t in range(4)]
         for t in range(4):
             cols = slice(t * P, (t + 1) * P)
             nc.tensor.matmul_mx(
                 out=acc1[t][:], lhsT=w1_codes[:, cols].bitcast(FP8X4), lhsT_scale=w1_scales[:, cols],
-                rhs=x_codes[:].bitcast(FP8X4), rhs_scale=plane1[:, :S], start=True, stop=True,
+                rhs=x_codes[:].bitcast(FP8X4), rhs_scale=x_plane[:], start=True, stop=True,
             )
 
-        picked2 = keep.tile([P, S], U8, name="picked2", tag="picked")
-        nc.vector.tensor_copy(picked2[:], d_bytes[:].indirect(k2_l[:]))
-        place_rows(plane2, picked2, (nc.sync,))
-        picked_w2 = keep.tile([P, S], U32, name="picked_w2", tag="picked")
+        picked_w2 = keep.tile([P, S], U32, name="picked_w2", tag="plane1")
         nc.vector.tensor_copy(picked_w2[:], d_tab[:].bitcast(U32).indirect(k2_l[:]))
         w2_codes = keep.tile([P, S], U32, name="w2_codes", align_bytes=64)
         w2_scales = keep.tile([P, S], U8, name="w2_scales", align_bytes=64)
-        deal(w2_codes[:], picked_w2[:])
-        deal(w2_scales[:], plane2[:])
+        deal(w2_codes[:], picked_w2[:], 8)
+        deal(w2_scales[:].bitcast(I32), plane2[:].bitcast(I32), 2)
 
         halves = [slice(0, HALF), slice(HALF, S)]
         lhalves = [slice(0, HCOLS), slice(HCOLS, 2 * HCOLS)]
@@ -113,27 +120,28 @@ def tile_picked_codeoverodds_none_p_kernel(
         for t in range(4):
             nc.scalar.activation(own[t][1][:], acc1[t][:, halves[1]], ACT.Copy, scale=0.75)
 
-        ex = [keep.tile([P, S], F32, name=f"ex{t}") for t in range(4)]
-        ex_own = [[keep.tile([P, HALF], F32, name=f"exown{t}_{c}") for c in range(2)] for t in range(4)]
-        arg = [None] + [keep.tile([P, S], F32, name=f"arg{t}", tag=f"arg{t}") for t in range(1, 4)]
+        ex_own = [keep.tile([P, S], F32, name=f"ex_own{t}") for t in range(4)]
         for c in range(2):
-            z_rows = keep.tile([P, 4, HALF], BF16, name=f"z_rows{c}")
+            z_pairs = keep.tile([P, 2, HALF, 2], BF16, name=f"z_pairs{c}", tag=f"z_pairs{c}")
+            early = keep.tile([P, 4 - 3 * c, 2, HALF], F32, name=f"early{c}")
+            late = early if c == 0 else keep.tile([P, 3, 2, HALF], F32, name="late", tag="z_packed0", align_bytes=64)
             for t in range(4):
-                u = ring.tile([P, HALF], F32, name="u")
-                v = ring.tile([P, HALF], F32, name="v")
-                m = ring.tile([P, HALF], F32, name="m")
-                nc.vector.tensor_tensor(u[:], h[t][:].indirect(n1_l[:, lhalves[c]]), own[t][c][:], ALU.subtract)
-                nc.vector.tensor_tensor(v[:], h[t][:].indirect(n2_l[:, lhalves[c]]), own[t][c][:], ALU.subtract)
-                nc.vector.tensor_tensor(m[:], u[:], v[:], ALU.max)
-                nc.scalar.activation(z_rows[:, t, :], m[:], ACT.Copy, scale=gain[:, t : t + 1])
-            z_packed = keep.tile([P, HALF, 4], BF16, name=f"z_packed{c}", align_bytes=64)
+                pair = early[:, t] if t < early.shape[1] else late[:, t - 1]
+                top = keep.tile([P, HALF], F32, name=f"top{t}_{c}")
+                nc.vector.tensor_tensor(pair[:, 0, :], h[t][:].indirect(n1_l[:, lhalves[c]]), own[t][c][:], ALU.subtract)
+                nc.vector.tensor_tensor(pair[:, 1, :], h[t][:].indirect(n2_l[:, lhalves[c]]), own[t][c][:], ALU.subtract)
+                nc.vector.tensor_tensor(top[:], pair[:, 0, :], pair[:, 1, :], ALU.max)
+                nc.scalar.activation(z_pairs[:, t // 2, :, t % 2], top[:], ACT.Copy, scale=gain[:, t : t + 1])
+            z_packed = keep.tile([P, HALF * 4], BF16, name=f"z_packed{c}", tag=f"z_packed{c}", align_bytes=64)
             weave = nc.scalar.copy if c == 0 else nc.vector.tensor_copy
-            weave(z_packed[:], z_rows[:].rearrange("p t j -> p j t"))
+            weave(
+                z_packed[:].bitcast(F32).rearrange("p (j u) -> p j u", u=2),
+                z_pairs[:].rearrange("p u j e -> p (u j e)").bitcast(F32).rearrange("p (u j) -> p j u", u=2),
+            )
             z_codes = keep.tile([P, HALF], U32, name=f"z_codes{c}", align_bytes=64)
             z_scales = keep.tile([P, HALF], U8, name=f"z_scales{c}", align_bytes=64)
-            nc.vector.quantize_mx(
-                out=z_codes[:].bitcast(FP8X4), scales=z_scales[:], in_=z_packed[:].rearrange("p j t -> p (j t)")
-            )
+            nc.vector.quantize_mx(out=z_codes[:].bitcast(FP8X4), scales=z_scales[:], in_=z_packed[:])
+            scale = first_scale[:] if c == 0 else 0.03125
             for t in range(4):
                 cols = slice(t * P, (t + 1) * P)
                 acc2 = psum.tile([P, HALF], F32, name=f"acc2_{t}_{c}", tag=f"high{t}" if c == 0 else f"low{t}")
@@ -141,38 +149,38 @@ def tile_picked_codeoverodds_none_p_kernel(
                     out=acc2[:], lhsT=w2_codes[:, cols].bitcast(FP8X4), lhsT_scale=w2_scales[:, cols],
                     rhs=z_codes[:].bitcast(FP8X4), rhs_scale=z_scales[:], start=True, stop=True,
                 )
-                nc.scalar.activation(ex[t][:, halves[c]], acc2[:], ACT.Exp, scale=0.03125)
-                nc.sync.dma_start(ex_own[t][c][:], ex[t][:, halves[c]])
-                if t > 0:
-                    nc.scalar.activation(arg[t][:, halves[c]], acc2[:], ACT.Copy, scale=0.03125)
+                nc.scalar.activation(ex[t][:, halves[c]], acc2[:], ACT.Exp, scale=scale)
+                nc.sync.dma_start(ex_own[t][:, halves[c]], ex[t][:, halves[c]])
+                if t in SCALAR_TILES:
+                    nc.scalar.activation(arg[t][:, halves[c]], acc2[:], ACT.Copy, scale=scale)
 
-        e4 = [[keep.tile([P, HALF], F32, name=f"e4_{t}_{c}") for c in range(2)] for t in range(4)]
-        for t in range(1, 4):
-            for c in range(2):
-                nc.scalar.activation(e4[t][c][:], arg[t][:].indirect(n4_l[:, lhalves[c]]), ACT.Exp)
-        for c in range(2):
-            nc.vector.tensor_copy(e4[0][c][:], ex[0][:].indirect(n4_l[:, lhalves[c]]))
+        e4 = [keep.tile([P, S], F32, name=f"e4_{t}") for t in range(4)]
+        for t in range(4):
+            if t in SCALAR_TILES:
+                nc.scalar.activation(e4[t][:], arg[t][:].indirect(n4_l[:]), ACT.Exp)
+            else:
+                nc.vector.tensor_copy(e4[t][:], ex[t][:].indirect(n4_l[:]))
 
         sums = [keep.tile([P, 2, S], F32, name=f"sums{t}") for t in range(4)]
 
-        def numer(t, c):
-            nc.vector.tensor_tensor(sums[t][:, 0, halves[c]], ex[t][:].indirect(n3_l[:, lhalves[c]]), ex_own[t][c][:], ALU.add)
+        def numer(t):
+            nc.vector.tensor_tensor(sums[t][:, 0, :], ex[t][:].indirect(n3_l[:]), ex_own[t][:], ALU.add)
 
-        def denom(t, c):
-            nc.vector.tensor_tensor(sums[t][:, 1, halves[c]], ex[t][:].indirect(n5_l[:, lhalves[c]]), e4[t][c][:], ALU.add)
+        def denom(t, cols, lcols):
+            nc.vector.tensor_tensor(sums[t][:, 1, cols], ex[t][:].indirect(n5_l[:, lcols]), e4[t][:, cols], ALU.add)
 
-        numer(0, 0)
-        denom(0, 0)
-        denom(0, 1)
-        numer(0, 1)
-        for t in range(1, 4):
-            for c in range(2):
-                numer(t, c)
-            for c in range(2):
-                denom(t, c)
+        whole = (slice(0, S), slice(0, 2 * HCOLS))
+        denom(0, *whole)
+        numer(0)
+        for t in range(1, 3):
+            numer(t)
+            denom(t, *whole)
+        numer(3)
+        for c in range(2):
+            denom(3, halves[c], lhalves[c])
 
         logs = keep.tile([P, 4, 2, S], F32, name="logs", tag="arg3")
-        rows = out.rearrange("(p t) j -> t p j", t=4)
+        rows = out.rearrange("(a t r) j -> t a r j", t=4, r=8)
         res = [keep.tile([P, S], F32, name=f"res{t}") for t in range(4)]
         for t in range(3):
             nc.scalar.activation(logs[:, t], sums[t][:], ACT.Ln)
@@ -182,4 +190,4 @@ def tile_picked_codeoverodds_none_p_kernel(
         for c in range(2):
             nc.scalar.activation(logs[:, 3, 1, halves[c]], sums[3][:, 1, halves[c]], ACT.Ln)
             nc.vector.tensor_tensor(res[3][:, halves[c]], logs[:, 3, 0, halves[c]], logs[:, 3, 1, halves[c]], ALU.subtract)
-            nc.sync.dma_start(rows[3][:, halves[c]], res[3][:, halves[c]])
+            nc.sync.dma_start(rows[3][:, :, halves[c]], res[3][:, halves[c]])

@@ -54,7 +54,7 @@ def tile_picked_codeoverodds_none_p_kernel(
         n5_l = load_list("n5_l", n5)
         n3_l = load_list("n3_l", n3)
 
-        plane1 = keep.tile([P, 2 * S], U8, name="plane1", tag="plane1")
+        plane1 = keep.tile([P, 2 * S], U8, name="plane1", tag="plane1", align_bytes=64)
         plane2 = keep.tile([P, S], U8, name="plane2")
         nc.vector.memset(plane1[:].bitcast(I32), 0)
         nc.vector.memset(plane2[:].bitcast(I32), 0)
@@ -62,8 +62,6 @@ def tile_picked_codeoverodds_none_p_kernel(
         nc.vector.memset(first_scale[:], 0.03125)
         ex = [keep.tile([P, 2 * S], F32, name=f"ex{t}") for t in range(4)]
         arg = {t: keep.tile([P, 2 * S], F32, name=f"arg{t}", tag=f"arg{t}") for t in SCALAR_TILES}
-        for window in ex + list(arg.values()):
-            nc.gpsimd.memset(window[:, S:], 0.0)
 
         gain = keep.tile([P, 4], F32, name="gain")
         nc.scalar.activation(gain[:], g_raw[:], ACT.Copy, scale=0.0625)
@@ -77,6 +75,11 @@ def tile_picked_codeoverodds_none_p_kernel(
                 dst.rearrange("p (t a r) -> p t a r", t=4, r=run), src.rearrange("p (a t r) -> p t a r", t=4, r=run)
             )
 
+        def deal_singly(dst, src, line):
+            nc.vector.tensor_copy(
+                dst.rearrange("p (t a m) -> p a t m", t=4, m=line), src.rearrange("p (a m t) -> p a t m", t=4, m=line)
+            )
+
         picked1 = keep.tile([P, 2 * S], U8, name="picked1")
         nc.vector.tensor_copy(picked1[:, :S], x_bytes[:].indirect(offs_l[:]))
         nc.vector.tensor_copy(picked1[:, S:], d_bytes[:].indirect(k1_l[:]))
@@ -86,14 +89,14 @@ def tile_picked_codeoverodds_none_p_kernel(
         place_rows(plane2, picked2)
         x_codes = keep.tile([P, S], U32, name="x_codes", align_bytes=64)
         nc.vector.tensor_copy(x_codes[:], x_tab[:].bitcast(U32).indirect(offs_l[:]))
-        picked_w1 = keep.tile([P, S], U32, name="picked_w1")
+        picked_w1 = keep.tile([P, S], U32, name="picked_w1", tag="picked_w")
         nc.vector.tensor_copy(picked_w1[:], d_tab[:].bitcast(U32).indirect(k1_l[:]))
-        w1_codes = keep.tile([P, S], U32, name="w1_codes", align_bytes=64)
+        w1_codes = keep.tile([P, S], U32, name="w1_codes", tag="plane1", align_bytes=64)
         w1_scales = keep.tile([P, S], U8, name="w1_scales", align_bytes=64)
-        deal(w1_codes[:], picked_w1[:], 1)
         x_plane = keep.tile([P, S], U8, name="x_plane", align_bytes=64)
         nc.vector.tensor_copy(x_plane[:].bitcast(I32), plane1[:, :S].bitcast(I32))
-        deal(w1_scales[:], plane1[:, S:], 1)
+        deal_singly(w1_scales[:], plane1[:, S:], 16)
+        deal_singly(w1_codes[:], picked_w1[:], 4)
 
         acc1 = [psum.tile([P, S], F32, name=f"acc1_{t}", tag=f"low{t}") for t in range(4)]
         for t in range(4):
@@ -103,35 +106,50 @@ def tile_picked_codeoverodds_none_p_kernel(
                 rhs=x_codes[:].bitcast(FP8X4), rhs_scale=x_plane[:], start=True, stop=True,
             )
 
-        picked_w2 = keep.tile([P, S], U32, name="picked_w2", tag="plane1")
+        picked_w2 = keep.tile([P, S], U32, name="picked_w2", tag="picked_w")
         nc.vector.tensor_copy(picked_w2[:], d_tab[:].bitcast(U32).indirect(k2_l[:]))
         w2_codes = keep.tile([P, S], U32, name="w2_codes", align_bytes=64)
         w2_scales = keep.tile([P, S], U8, name="w2_scales", align_bytes=64)
-        deal(w2_codes[:], picked_w2[:], 8)
         deal(w2_scales[:].bitcast(I32), plane2[:].bitcast(I32), 2)
+        deal(w2_codes[:], picked_w2[:], 8)
 
         halves = [slice(0, HALF), slice(HALF, S)]
         lhalves = [slice(0, HCOLS), slice(HCOLS, 2 * HCOLS)]
         h = [keep.tile([P, S], F32, name=f"h{t}") for t in range(4)]
-        own = [[keep.tile([P, HALF], F32, name=f"own{t}_{c}") for c in range(2)] for t in range(4)]
+        own = [[ex[t][:, S + c * HALF : S + (c + 1) * HALF] for c in range(2)] for t in range(4)]
         for t in range(4):
             nc.scalar.copy(h[t][:], acc1[t][:])
-            nc.scalar.activation(own[t][0][:], acc1[t][:, halves[0]], ACT.Copy, scale=0.75)
+            nc.scalar.activation(own[t][0], acc1[t][:, halves[0]], ACT.Copy, scale=0.75)
         for t in range(4):
-            nc.scalar.activation(own[t][1][:], acc1[t][:, halves[1]], ACT.Copy, scale=0.75)
+            nc.scalar.activation(own[t][1], acc1[t][:, halves[1]], ACT.Copy, scale=0.75)
 
+        first_pair = keep.tile([P, S], F32, name="first_pair")
         ex_own = [keep.tile([P, S], F32, name=f"ex_own{t}") for t in range(4)]
         for c in range(2):
             z_pairs = keep.tile([P, 2, HALF, 2], BF16, name=f"z_pairs{c}", tag=f"z_pairs{c}")
-            early = keep.tile([P, 4 - 3 * c, 2, HALF], F32, name=f"early{c}")
-            late = early if c == 0 else keep.tile([P, 3, 2, HALF], F32, name="late", tag="z_packed0", align_bytes=64)
-            for t in range(4):
-                pair = early[:, t] if t < early.shape[1] else late[:, t - 1]
-                top = keep.tile([P, HALF], F32, name=f"top{t}_{c}")
-                nc.vector.tensor_tensor(pair[:, 0, :], h[t][:].indirect(n1_l[:, lhalves[c]]), own[t][c][:], ALU.subtract)
-                nc.vector.tensor_tensor(pair[:, 1, :], h[t][:].indirect(n2_l[:, lhalves[c]]), own[t][c][:], ALU.subtract)
-                nc.vector.tensor_tensor(top[:], pair[:, 0, :], pair[:, 1, :], ALU.max)
-                nc.scalar.activation(z_pairs[:, t // 2, :, t % 2], top[:], ACT.Copy, scale=gain[:, t : t + 1])
+            if c == 0:
+                slots = [first_pair[:, :HALF], first_pair[:, HALF:]]
+                slots += [arg[t][:, S + e * HALF : S + (e + 1) * HALF] for t in range(1, 4) for e in range(2)]
+            else:
+                early = keep.tile([P, 3, HALF], F32, name="early")
+                late = keep.tile([P, 5, HALF], F32, name="late", tag="z_packed0", align_bytes=64)
+                slots = [early[:, i, :] for i in range(3)] + [late[:, i, :] for i in range(5)]
+            last_top = keep.tile([P, HALF], F32, name=f"last_top{c}")
+            tops = [own[1][c], own[2][c], own[3][c], last_top[:]]
+
+            def fetch(t):
+                nc.vector.tensor_tensor(slots[2 * t], h[t][:].indirect(n1_l[:, lhalves[c]]), own[t][c], ALU.subtract)
+                nc.vector.tensor_tensor(slots[2 * t + 1], h[t][:].indirect(n2_l[:, lhalves[c]]), own[t][c], ALU.subtract)
+
+            def larger(t):
+                nc.vector.tensor_tensor(tops[t], slots[2 * t], slots[2 * t + 1], ALU.max)
+                nc.scalar.activation(z_pairs[:, t // 2, :, t % 2], tops[t], ACT.Copy, scale=gain[:, t : t + 1])
+
+            fetch(0)
+            for t in range(1, 4):
+                fetch(t)
+                larger(t - 1)
+            larger(3)
             z_packed = keep.tile([P, HALF * 4], BF16, name=f"z_packed{c}", tag=f"z_packed{c}", align_bytes=64)
             weave = nc.scalar.copy if c == 0 else nc.vector.tensor_copy
             weave(
@@ -163,19 +181,20 @@ def tile_picked_codeoverodds_none_p_kernel(
 
         sums = [keep.tile([P, 2, S], F32, name=f"sums{t}") for t in range(4)]
 
-        def numer(t):
-            nc.vector.tensor_tensor(sums[t][:, 0, :], ex[t][:].indirect(n3_l[:]), ex_own[t][:], ALU.add)
+        def numer(t, cols, lcols):
+            nc.vector.tensor_tensor(sums[t][:, 0, cols], ex[t][:].indirect(n3_l[:, lcols]), ex_own[t][:, cols], ALU.add)
 
         def denom(t, cols, lcols):
             nc.vector.tensor_tensor(sums[t][:, 1, cols], ex[t][:].indirect(n5_l[:, lcols]), e4[t][:, cols], ALU.add)
 
         whole = (slice(0, S), slice(0, 2 * HCOLS))
+        numer(0, halves[0], lhalves[0])
         denom(0, *whole)
-        numer(0)
+        numer(0, halves[1], lhalves[1])
         for t in range(1, 3):
-            numer(t)
+            numer(t, *whole)
             denom(t, *whole)
-        numer(3)
+        numer(3, *whole)
         for c in range(2):
             denom(3, halves[c], lhalves[c])
 

@@ -117,60 +117,117 @@ def tile_picked_codeoverodds_none_p_kernel(
         lhalves = [slice(0, HCOLS), slice(HCOLS, 2 * HCOLS)]
         h = [keep.tile([P, S], F32, name=f"h{t}") for t in range(4)]
         own = [[ex[t][:, S + c * HALF : S + (c + 1) * HALF] for c in range(2)] for t in range(4)]
+        own_first = {t: keep.tile([P, HALF], F32, name=f"own_first{t}") for t in range(1, 4)}
         for t in range(4):
             nc.scalar.copy(h[t][:], acc1[t][:])
+            if t > 0:
+                nc.scalar.activation(own_first[t][:], acc1[t][:, halves[0]], ACT.Copy, scale=0.75)
             nc.scalar.activation(own[t][0], acc1[t][:, halves[0]], ACT.Copy, scale=0.75)
         for t in range(4):
             nc.scalar.activation(own[t][1], acc1[t][:, halves[1]], ACT.Copy, scale=0.75)
 
         first_pair = keep.tile([P, S], F32, name="first_pair")
         ex_own = [keep.tile([P, S], F32, name=f"ex_own{t}") for t in range(4)]
-        for c in range(2):
-            z_pairs = keep.tile([P, 2, HALF, 2], BF16, name=f"z_pairs{c}", tag=f"z_pairs{c}")
-            if c == 0:
-                slots = [first_pair[:, :HALF], first_pair[:, HALF:]]
-                slots += [arg[t][:, S + e * HALF : S + (e + 1) * HALF] for t in range(1, 4) for e in range(2)]
-            else:
-                early = keep.tile([P, 3, HALF], F32, name="early")
-                late = keep.tile([P, 5, HALF], F32, name="late", tag="z_packed0", align_bytes=64)
-                slots = [early[:, i, :] for i in range(3)] + [late[:, i, :] for i in range(5)]
-            last_top = keep.tile([P, HALF], F32, name=f"last_top{c}")
-            tops = [own[1][c], own[2][c], own[3][c], last_top[:]]
 
-            def fetch(t):
-                nc.vector.tensor_tensor(slots[2 * t], h[t][:].indirect(n1_l[:, lhalves[c]]), own[t][c], ALU.subtract)
-                nc.vector.tensor_tensor(slots[2 * t + 1], h[t][:].indirect(n2_l[:, lhalves[c]]), own[t][c], ALU.subtract)
+        def fetch(dst, t, lst, cols, sub):
+            nc.vector.tensor_tensor(dst, h[t][:].indirect(lst[:, cols.start // 16 : cols.stop // 16]), sub, ALU.subtract)
 
-            def larger(t):
-                nc.vector.tensor_tensor(tops[t], slots[2 * t], slots[2 * t + 1], ALU.max)
-                nc.scalar.activation(z_pairs[:, t // 2, :, t % 2], tops[t], ACT.Copy, scale=gain[:, t : t + 1])
-
-            fetch(0)
-            for t in range(1, 4):
-                fetch(t)
-                larger(t - 1)
-            larger(3)
-            z_packed = keep.tile([P, HALF * 4], BF16, name=f"z_packed{c}", tag=f"z_packed{c}", align_bytes=64)
-            weave = nc.scalar.copy if c == 0 else nc.vector.tensor_copy
-            weave(
-                z_packed[:].bitcast(F32).rearrange("p (j u) -> p j u", u=2),
-                z_pairs[:].rearrange("p u j e -> p (u j e)").bitcast(F32).rearrange("p (u j) -> p j u", u=2),
+        def weave(engine_copy, packed, pairs):
+            engine_copy(
+                packed.bitcast(F32).rearrange("p (j u) -> p j u", u=2),
+                pairs.rearrange("p u j e -> p (u j e)").bitcast(F32).rearrange("p (u j) -> p j u", u=2),
             )
-            z_codes = keep.tile([P, HALF], U32, name=f"z_codes{c}", align_bytes=64)
-            z_scales = keep.tile([P, HALF], U8, name=f"z_scales{c}", align_bytes=64)
-            nc.vector.quantize_mx(out=z_codes[:].bitcast(FP8X4), scales=z_scales[:], in_=z_packed[:])
-            scale = first_scale[:] if c == 0 else 0.03125
-            for t in range(4):
-                cols = slice(t * P, (t + 1) * P)
-                acc2 = psum.tile([P, HALF], F32, name=f"acc2_{t}_{c}", tag=f"high{t}" if c == 0 else f"low{t}")
-                nc.tensor.matmul_mx(
-                    out=acc2[:], lhsT=w2_codes[:, cols].bitcast(FP8X4), lhsT_scale=w2_scales[:, cols],
-                    rhs=z_codes[:].bitcast(FP8X4), rhs_scale=z_scales[:], start=True, stop=True,
-                )
-                nc.scalar.activation(ex[t][:, halves[c]], acc2[:], ACT.Exp, scale=scale)
-                nc.sync.dma_start(ex_own[t][:, halves[c]], ex[t][:, halves[c]])
-                if t in SCALAR_TILES:
-                    nc.scalar.activation(arg[t][:, halves[c]], acc2[:], ACT.Copy, scale=scale)
+
+        def product(acc, t, codes, scales):
+            cols = slice(t * P, (t + 1) * P)
+            nc.tensor.matmul_mx(
+                out=acc, lhsT=w2_codes[:, cols].bitcast(FP8X4), lhsT_scale=w2_scales[:, cols],
+                rhs=codes.bitcast(FP8X4), rhs_scale=scales, start=True, stop=True,
+            )
+
+        def leave(acc, t, cols, scale):
+            nc.scalar.activation(ex[t][:, cols], acc, ACT.Exp, scale=scale)
+            nc.sync.dma_start(ex_own[t][:, cols], ex[t][:, cols])
+            if t in SCALAR_TILES:
+                nc.scalar.activation(arg[t][:, cols], acc, ACT.Copy, scale=scale)
+
+        z_codes = keep.tile([P, S], U32, name="z_codes", align_bytes=64)
+        z_scales = keep.tile([P, S], U8, name="z_scales", align_bytes=64)
+
+        def quantise(cols, packed):
+            nc.vector.quantize_mx(out=z_codes[:, cols].bitcast(FP8X4), scales=z_scales[:, cols], in_=packed)
+
+        pairs0 = keep.tile([P, 2, HALF, 2], BF16, name="pairs0", tag="z_pairs0")
+        slots = [first_pair[:, :HALF], first_pair[:, HALF:]]
+        slots += [arg[t][:, S + e * HALF : S + (e + 1) * HALF] for t in range(1, 4) for e in range(2)]
+        last_top = keep.tile([P, HALF], F32, name="last_top")
+        tops = [own_first[1][:], own_first[2][:], own_first[3][:], last_top[:]]
+        subs = [own[0][0]] + [own_first[t][:] for t in range(1, 4)]
+
+        def larger0(t):
+            nc.vector.tensor_tensor(tops[t], slots[2 * t], slots[2 * t + 1], ALU.max)
+            nc.scalar.activation(pairs0[:, t // 2, :, t % 2], tops[t], ACT.Copy, scale=gain[:, t : t + 1])
+
+        for t in range(4):
+            fetch(slots[2 * t], t, n1_l, halves[0], subs[t])
+            fetch(slots[2 * t + 1], t, n2_l, halves[0], own[t][0])
+            if t > 0:
+                larger0(t - 1)
+        larger0(3)
+        packed0 = keep.tile([P, HALF * 4], BF16, name="packed0", tag="z_packed0", align_bytes=64)
+        weave(nc.scalar.copy, packed0[:], pairs0[:])
+        quantise(halves[0], packed0[:])
+        for t in range(4):
+            acc = psum.tile([P, HALF], F32, name=f"acc2_{t}_0", tag=f"high{t}")
+            product(acc[:], t, z_codes[:, halves[0]], z_scales[:, halves[0]])
+            leave(acc[:], t, halves[0], first_scale[:])
+
+        Q = HALF // 2
+        pairs1 = keep.tile([P, 2, 2, Q, 2], BF16, name="pairs1", tag="z_pairs1")
+        early = keep.tile([P, 3, HALF], F32, name="early")
+        late = keep.tile([P, 5, HALF], F32, name="late", tag="z_packed0", align_bytes=64)
+        slots1 = [early[:, i, :] for i in range(3)] + [late[:, i, :] for i in range(5)]
+        tops1 = [keep.tile([P, HALF], F32, name=f"top{t}", tag="z_pairs0" if t == 0 else f"top{t}") for t in range(4)]
+
+        def larger1(t):
+            nc.vector.tensor_tensor(tops1[t][:], slots1[2 * t], slots1[2 * t + 1], ALU.max)
+            nc.scalar.activation(
+                pairs1[:, :, t // 2, :, t % 2], tops1[t][:].rearrange("p (q j) -> p q j", q=2), ACT.Copy, scale=gain[:, t : t + 1]
+            )
+
+        def last_fetch(e, q):
+            part = slice(q * Q, (q + 1) * Q)
+            fetch(slots1[6 + e][:, part], 3, (n1_l, n2_l)[e], slice(HALF + q * Q, HALF + (q + 1) * Q), own[3][1][:, part])
+
+        def last_larger(q):
+            part = slice(q * Q, (q + 1) * Q)
+            nc.vector.tensor_tensor(tops1[3][:, part], slots1[6][:, part], slots1[7][:, part], ALU.max)
+            nc.scalar.activation(pairs1[:, q, 1, :, 1], tops1[3][:, part], ACT.Copy, scale=gain[:, 3:4])
+
+        for t in range(3):
+            fetch(slots1[2 * t], t, n1_l, halves[1], own[t][1])
+            if t > 0:
+                larger1(t - 1)
+            fetch(slots1[2 * t + 1], t, n2_l, halves[1], own[t][1])
+        last_fetch(0, 0)
+        larger1(2)
+        last_fetch(1, 0)
+        last_fetch(0, 1)
+        last_larger(0)
+        last_fetch(1, 1)
+        packed1 = [keep.tile([P, Q * 4], BF16, name=f"packed1_{q}", align_bytes=64) for q in range(2)]
+        quarters = [slice(HALF + q * Q, HALF + (q + 1) * Q) for q in range(2)]
+        weave(nc.vector.tensor_copy, packed1[0][:], pairs1[:, 0])
+        last_larger(1)
+        quantise(quarters[0], packed1[0][:])
+        accs = [psum.tile([P, HALF], F32, name=f"acc2_{t}_1", tag=f"low{t}") for t in range(4)]
+        for t in range(4):
+            product(accs[t][:, :Q], t, z_codes[:, quarters[0]], z_scales[:, quarters[0]])
+        weave(nc.vector.tensor_copy, packed1[1][:], pairs1[:, 1])
+        quantise(quarters[1], packed1[1][:])
+        for t in range(4):
+            product(accs[t][:, Q:], t, z_codes[:, quarters[1]], z_scales[:, quarters[1]])
+            leave(accs[t][:], t, halves[1], 0.03125)
 
         e4 = [keep.tile([P, S], F32, name=f"e4_{t}") for t in range(4)]
         for t in range(4):
@@ -179,34 +236,42 @@ def tile_picked_codeoverodds_none_p_kernel(
             else:
                 nc.vector.tensor_copy(e4[t][:], ex[t][:].indirect(n4_l[:]))
 
-        sums = [keep.tile([P, 2, S], F32, name=f"sums{t}") for t in range(4)]
+        sums = [keep.tile([P, 2, S], F32, name=f"sums{t}") for t in range(3)]
 
-        def numer(t, cols, lcols):
-            nc.vector.tensor_tensor(sums[t][:, 0, cols], ex[t][:].indirect(n3_l[:, lcols]), ex_own[t][:, cols], ALU.add)
+        def numer(t, cols, lcols, dst):
+            nc.vector.tensor_tensor(dst, ex[t][:].indirect(n3_l[:, lcols]), ex_own[t][:, cols], ALU.add)
 
-        def denom(t, cols, lcols):
-            nc.vector.tensor_tensor(sums[t][:, 1, cols], ex[t][:].indirect(n5_l[:, lcols]), e4[t][:, cols], ALU.add)
+        def denom(t, cols, lcols, dst):
+            nc.vector.tensor_tensor(dst, ex[t][:].indirect(n5_l[:, lcols]), e4[t][:, cols], ALU.add)
 
         whole = (slice(0, S), slice(0, 2 * HCOLS))
-        numer(0, halves[0], lhalves[0])
-        denom(0, *whole)
-        numer(0, halves[1], lhalves[1])
+        numer(0, halves[0], lhalves[0], sums[0][:, 0, halves[0]])
+        denom(0, *whole, sums[0][:, 1, :])
+        numer(0, halves[1], lhalves[1], sums[0][:, 0, halves[1]])
         for t in range(1, 3):
-            numer(t, *whole)
-            denom(t, *whole)
-        numer(3, *whole)
-        for c in range(2):
-            denom(3, halves[c], lhalves[c])
+            numer(t, *whole, sums[t][:, 0, :])
+            denom(t, *whole, sums[t][:, 1, :])
+        last_numer = keep.tile([P, S], F32, name="last_numer")
+        numer(3, *whole, last_numer[:])
 
         logs = keep.tile([P, 4, 2, S], F32, name="logs", tag="arg3")
         rows = out.rearrange("(a t r) j -> t a r j", t=4, r=8)
         res = [keep.tile([P, S], F32, name=f"res{t}") for t in range(4)]
-        for t in range(3):
-            nc.scalar.activation(logs[:, t], sums[t][:], ACT.Ln)
-            nc.vector.tensor_tensor(res[t][:], logs[:, t, 0, :], logs[:, t, 1, :], ALU.subtract)
-            nc.sync.dma_start(rows[t], res[t][:])
-        nc.scalar.activation(logs[:, 3, 0, :], sums[3][:, 0, :], ACT.Ln)
-        for c in range(2):
-            nc.scalar.activation(logs[:, 3, 1, halves[c]], sums[3][:, 1, halves[c]], ACT.Ln)
-            nc.vector.tensor_tensor(res[3][:, halves[c]], logs[:, 3, 0, halves[c]], logs[:, 3, 1, halves[c]], ALU.subtract)
-            nc.sync.dma_start(rows[3][:, :, halves[c]], res[3][:, halves[c]])
+
+        def finish(t, cols):
+            nc.vector.tensor_tensor(res[t][:, cols], logs[:, t, 0, cols], logs[:, t, 1, cols], ALU.subtract)
+            nc.sync.dma_start(rows[t][:, :, cols], res[t][:, cols])
+
+        nc.scalar.activation(logs[:, 0], sums[0][:], ACT.Ln)
+        finish(0, whole[0])
+        denom(3, halves[1], lhalves[1], sums[0][:, 0, halves[1]])
+        nc.scalar.activation(logs[:, 1], sums[1][:], ACT.Ln)
+        finish(1, whole[0])
+        denom(3, halves[0], lhalves[0], sums[1][:, 0, halves[0]])
+        nc.scalar.activation(logs[:, 2], sums[2][:], ACT.Ln)
+        nc.scalar.activation(logs[:, 3, 0, :], last_numer[:], ACT.Ln)
+        nc.scalar.activation(logs[:, 3, 1, halves[1]], sums[0][:, 0, halves[1]], ACT.Ln)
+        nc.scalar.activation(logs[:, 3, 1, halves[0]], sums[1][:, 0, halves[0]], ACT.Ln)
+        finish(2, whole[0])
+        finish(3, halves[1])
+        finish(3, halves[0])

from contextlib import ExitStack

import concourse.mybir as mybir

F32 = mybir.dt.float32
BF16 = mybir.dt.bfloat16
I32 = mybir.dt.int32
U32 = mybir.dt.uint32
U16 = mybir.dt.uint16
U8 = mybir.dt.uint8
FP8X4 = mybir.dt.float8_e4m3fn_x4
ALU = mybir.AluOpType
ACT = mybir.ActivationFunctionType

P = 128
T, G, S = 1024, 2048, 512
HALF = S // 2
HCOLS = HALF // 16
SCALAR_TILES = (1, 2, 3)
FLOPS = 2 * 2 * 512 * 512 * 512


def tile_picked_codeoverodds_none_p_kernel(
    tc, x_words, x_scales, d_words, d_scales, gs, offs, k1, n1, n2, k2, n3, n4, n5, out
):
    nc = tc.nc
    with ExitStack() as ctx:
        lists = ctx.enter_context(tc.tile_pool(name="lists", bufs=1))
        keep = ctx.enter_context(tc.tile_pool(name="keep", bufs=1))
        psum = ctx.enter_context(tc.psum_pool(name="psum", bufs=1))

        def load_list(name, src):
            tile = lists.tile([P, S // 16], U16, name=name)
            nc.sync.dma_start(tile[:], src)
            return tile

        d_bytes = keep.tile([P, G], U8, name="d_bytes")
        x_bytes = keep.tile([P, T], U8, name="x_bytes")
        x_tab = keep.tile([P, T], I32, name="x_tab")
        d_tab = keep.tile([P, G], I32, name="d_tab")
        g_raw = keep.tile([P, 4], F32, name="g_raw")

        offs_l = load_list("offs_l", offs)
        nc.sync.dma_start(x_bytes[:].bitcast(I32), x_scales[0].bitcast(I32).unsqueeze(1).to_broadcast([16, 8, T // 4]))
        k1_l = load_list("k1_l", k1)
        nc.sync.dma_start(d_bytes[:].bitcast(I32), d_scales[0].bitcast(I32).unsqueeze(1).to_broadcast([16, 8, G // 4]))
        k2_l = load_list("k2_l", k2)
        nc.sync.dma_start(x_tab[:], x_words[0].rearrange("p n t -> p (n t)").bitcast(I32))
        n1_l = load_list("n1_l", n1)
        n2_l = load_list("n2_l", n2)
        nc.sync.dma_start(g_raw[:], gs.rearrange("(p t) o -> p (t o)", t=4))
        nc.sync.dma_start(d_tab[:], d_words[0].rearrange("p n t -> p (n t)").bitcast(I32))
        n4_l = load_list("n4_l", n4)
        n5_l = load_list("n5_l", n5)
        n3_l = load_list("n3_l", n3)

        plane1 = keep.tile([P, 2 * S], U8, name="plane1", tag="plane1", align_bytes=64)
        plane2 = keep.tile([P, S], U8, name="plane2")
        nc.vector.memset(plane1[:].bitcast(I32), 0)
        nc.vector.memset(plane2[:].bitcast(I32), 0)
        first_scale = keep.tile([P, 1], F32, name="first_scale", tag="z_pairs1")
        nc.vector.memset(first_scale[:], 0.03125)
        ex = [keep.tile([P, 2 * S], F32, name=f"ex{t}") for t in range(4)]
        arg = {t: keep.tile([P, 2 * S], F32, name=f"arg{t}", tag=f"arg{t}") for t in SCALAR_TILES}

        gain = keep.tile([P, 4], F32, name="gain")
        nc.scalar.activation(gain[:], g_raw[:], ACT.Copy, scale=0.0625)

        def place_rows(plane, picked):
            for j in range(4):
                nc.sync.dma_start(plane[:].bitcast(I32)[j:P:32, :], picked[:].bitcast(I32)[8 * j : P : 32, :])

        def deal(dst, src, run):
            nc.vector.tensor_copy(
                dst.rearrange("p (t a r) -> p t a r", t=4, r=run), src.rearrange("p (a t r) -> p t a r", t=4, r=run)
            )

        def deal_singly(dst, src, line):
            nc.vector.tensor_copy(
                dst.rearrange("p (t a m) -> p a t m", t=4, m=line), src.rearrange("p (a m t) -> p a t m", t=4, m=line)
            )

        picked1 = keep.tile([P, 2 * S], U8, name="picked1")
        nc.vector.tensor_copy(picked1[:, :S], x_bytes[:].indirect(offs_l[:]))
        nc.vector.tensor_copy(picked1[:, S:], d_bytes[:].indirect(k1_l[:]))
        place_rows(plane1, picked1)
        picked2 = keep.tile([P, S], U8, name="picked2")
        nc.vector.tensor_copy(picked2[:], d_bytes[:].indirect(k2_l[:]))
        place_rows(plane2, picked2)
        x_codes = keep.tile([P, S], U32, name="x_codes", align_bytes=64)
        nc.vector.tensor_copy(x_codes[:], x_tab[:].bitcast(U32).indirect(offs_l[:]))
        picked_w1 = keep.tile([P, S], U32, name="picked_w1", tag="picked_w")
        nc.vector.tensor_copy(picked_w1[:], d_tab[:].bitcast(U32).indirect(k1_l[:]))
        w1_codes = keep.tile([P, S], U32, name="w1_codes", tag="plane1", align_bytes=64)
        w1_scales = keep.tile([P, S], U8, name="w1_scales", align_bytes=64)
        x_plane = keep.tile([P, S], U8, name="x_plane", align_bytes=64)
        nc.vector.tensor_copy(x_plane[:].bitcast(I32), plane1[:, :S].bitcast(I32))
        deal_singly(w1_scales[:], plane1[:, S:], 16)
        deal_singly(w1_codes[:], picked_w1[:], 4)

        acc1 = [psum.tile([P, S], F32, name=f"acc1_{t}", tag=f"low{t}") for t in range(4)]
        for t in range(4):
            cols = slice(t * P, (t + 1) * P)
            nc.tensor.matmul_mx(
                out=acc1[t][:], lhsT=w1_codes[:, cols].bitcast(FP8X4), lhsT_scale=w1_scales[:, cols],
                rhs=x_codes[:].bitcast(FP8X4), rhs_scale=x_plane[:], start=True, stop=True,
            )

        picked_w2 = keep.tile([P, S], U32, name="picked_w2", tag="picked_w")
        nc.vector.tensor_copy(picked_w2[:], d_tab[:].bitcast(U32).indirect(k2_l[:]))
        w2_codes = keep.tile([P, S], U32, name="w2_codes", align_bytes=64)
        w2_scales = keep.tile([P, S], U8, name="w2_scales", align_bytes=64)
        deal(w2_scales[:].bitcast(I32), plane2[:].bitcast(I32), 2)
        deal(w2_codes[:], picked_w2[:], 8)

        halves = [slice(0, HALF), slice(HALF, S)]
        lhalves = [slice(0, HCOLS), slice(HCOLS, 2 * HCOLS)]
        h = [keep.tile([P, S], F32, name=f"h{t}") for t in range(4)]
        own = [[ex[t][:, S + c * HALF : S + (c + 1) * HALF] for c in range(2)] for t in range(4)]
        own_first = {t: keep.tile([P, HALF], F32, name=f"own_first{t}") for t in range(1, 4)}
        for t in range(4):
            nc.scalar.copy(h[t][:], acc1[t][:])
            if t > 0:
                nc.scalar.activation(own_first[t][:], acc1[t][:, halves[0]], ACT.Copy, scale=0.75)
            nc.scalar.activation(own[t][0], acc1[t][:, halves[0]], ACT.Copy, scale=0.75)
        for t in range(4):
            nc.scalar.activation(own[t][1], acc1[t][:, halves[1]], ACT.Copy, scale=0.75)

        first_pair = keep.tile([P, S], F32, name="first_pair")
        ex_own = [keep.tile([P, S], F32, name=f"ex_own{t}") for t in range(4)]

        def fetch(dst, t, lst, cols, sub):
            nc.vector.tensor_tensor(dst, h[t][:].indirect(lst[:, cols.start // 16 : cols.stop // 16]), sub, ALU.subtract)

        def weave(engine_copy, packed, pairs):
            engine_copy(
                packed.bitcast(F32).rearrange("p (j u) -> p j u", u=2),
                pairs.rearrange("p u j e -> p (u j e)").bitcast(F32).rearrange("p (u j) -> p j u", u=2),
            )

        def product(acc, t, codes, scales):
            cols = slice(t * P, (t + 1) * P)
            nc.tensor.matmul_mx(
                out=acc, lhsT=w2_codes[:, cols].bitcast(FP8X4), lhsT_scale=w2_scales[:, cols],
                rhs=codes.bitcast(FP8X4), rhs_scale=scales, start=True, stop=True,
            )

        def leave(acc, t, cols, scale):
            nc.scalar.activation(ex[t][:, cols], acc, ACT.Exp, scale=scale)
            nc.sync.dma_start(ex_own[t][:, cols], ex[t][:, cols])
            if t in SCALAR_TILES:
                nc.scalar.activation(arg[t][:, cols], acc, ACT.Copy, scale=scale)

        z_codes = keep.tile([P, S], U32, name="z_codes", align_bytes=64)
        z_scales = keep.tile([P, S], U8, name="z_scales", align_bytes=64)

        def quantise(cols, packed):
            nc.vector.quantize_mx(out=z_codes[:, cols].bitcast(FP8X4), scales=z_scales[:, cols], in_=packed)

        pairs0 = keep.tile([P, 2, HALF, 2], BF16, name="pairs0", tag="z_pairs0")
        slots = [first_pair[:, :HALF], first_pair[:, HALF:]]
        slots += [arg[t][:, S + e * HALF : S + (e + 1) * HALF] for t in range(1, 4) for e in range(2)]
        last_top = keep.tile([P, HALF], F32, name="last_top")
        tops = [own_first[1][:], own_first[2][:], own_first[3][:], last_top[:]]
        subs = [own[0][0]] + [own_first[t][:] for t in range(1, 4)]

        def larger0(t):
            nc.vector.tensor_tensor(tops[t], slots[2 * t], slots[2 * t + 1], ALU.max)
            nc.scalar.activation(pairs0[:, t // 2, :, t % 2], tops[t], ACT.Copy, scale=gain[:, t : t + 1])

        for t in range(4):
            fetch(slots[2 * t], t, n1_l, halves[0], subs[t])
            fetch(slots[2 * t + 1], t, n2_l, halves[0], own[t][0])
            if t > 0:
                larger0(t - 1)
        larger0(3)
        packed0 = keep.tile([P, HALF * 4], BF16, name="packed0", tag="z_packed0", align_bytes=64)
        weave(nc.scalar.copy, packed0[:], pairs0[:])
        quantise(halves[0], packed0[:])
        for t in range(4):
            acc = psum.tile([P, HALF], F32, name=f"acc2_{t}_0", tag=f"high{t}")
            product(acc[:], t, z_codes[:, halves[0]], z_scales[:, halves[0]])
            leave(acc[:], t, halves[0], first_scale[:])

        Q = HALF // 2
        pairs1 = keep.tile([P, 2, 2, Q, 2], BF16, name="pairs1", tag="z_pairs1")
        early = keep.tile([P, 3, HALF], F32, name="early")
        late = keep.tile([P, 5, HALF], F32, name="late", tag="z_packed0", align_bytes=64)
        slots1 = [early[:, i, :] for i in range(3)] + [late[:, i, :] for i in range(5)]
        tops1 = [keep.tile([P, HALF], F32, name=f"top{t}", tag="z_pairs0" if t == 0 else f"top{t}") for t in range(4)]

        def larger1(t):
            nc.vector.tensor_tensor(tops1[t][:], slots1[2 * t], slots1[2 * t + 1], ALU.max)
            nc.scalar.activation(
                pairs1[:, :, t // 2, :, t % 2], tops1[t][:].rearrange("p (q j) -> p q j", q=2), ACT.Copy, scale=gain[:, t : t + 1]
            )

        def last_fetch(e, q):
            part = slice(q * Q, (q + 1) * Q)
            fetch(slots1[6 + e][:, part], 3, (n1_l, n2_l)[e], slice(HALF + q * Q, HALF + (q + 1) * Q), own[3][1][:, part])

        def last_larger(q):
            part = slice(q * Q, (q + 1) * Q)
            nc.vector.tensor_tensor(tops1[3][:, part], slots1[6][:, part], slots1[7][:, part], ALU.max)
            nc.scalar.activation(pairs1[:, q, 1, :, 1], tops1[3][:, part], ACT.Copy, scale=gain[:, 3:4])

        for t in range(3):
            fetch(slots1[2 * t], t, n1_l, halves[1], own[t][1])
            if t > 0:
                larger1(t - 1)
            fetch(slots1[2 * t + 1], t, n2_l, halves[1], own[t][1])
        last_fetch(0, 0)
        larger1(2)
        last_fetch(1, 0)
        last_fetch(0, 1)
        last_larger(0)
        last_fetch(1, 1)
        packed1 = [keep.tile([P, Q * 4], BF16, name=f"packed1_{q}", align_bytes=64) for q in range(2)]
        quarters = [slice(HALF + q * Q, HALF + (q + 1) * Q) for q in range(2)]
        weave(nc.vector.tensor_copy, packed1[0][:], pairs1[:, 0])
        last_larger(1)
        quantise(quarters[0], packed1[0][:])
        accs = [psum.tile([P, HALF], F32, name=f"acc2_{t}_1", tag=f"low{t}") for t in range(4)]
        for t in range(4):
            product(accs[t][:, :Q], t, z_codes[:, quarters[0]], z_scales[:, quarters[0]])
        weave(nc.vector.tensor_copy, packed1[1][:], pairs1[:, 1])
        quantise(quarters[1], packed1[1][:])
        for t in range(4):
            product(accs[t][:, Q:], t, z_codes[:, quarters[1]], z_scales[:, quarters[1]])
            leave(accs[t][:], t, halves[1], 0.03125)

        e4 = [keep.tile([P, S], F32, name=f"e4_{t}") for t in range(4)]
        for t in range(4):
            if t in SCALAR_TILES:
                nc.scalar.activation(e4[t][:], arg[t][:].indirect(n4_l[:]), ACT.Exp)
            else:
                nc.vector.tensor_copy(e4[t][:], ex[t][:].indirect(n4_l[:]))

        sums = [keep.tile([P, 2, S], F32, name=f"sums{t}") for t in range(3)]

        def numer(t, cols, lcols, dst):
            nc.vector.tensor_tensor(dst, ex[t][:].indirect(n3_l[:, lcols]), ex_own[t][:, cols], ALU.add)

        def denom(t, cols, lcols, dst):
            nc.vector.tensor_tensor(dst, ex[t][:].indirect(n5_l[:, lcols]), e4[t][:, cols], ALU.add)

        whole = (slice(0, S), slice(0, 2 * HCOLS))
        numer(0, halves[0], lhalves[0], sums[0][:, 0, halves[0]])
        denom(0, *whole, sums[0][:, 1, :])
        numer(0, halves[1], lhalves[1], sums[0][:, 0, halves[1]])
        for t in range(1, 3):
            numer(t, *whole, sums[t][:, 0, :])
            denom(t, *whole, sums[t][:, 1, :])
        last_numer = keep.tile([P, S], F32, name="last_numer")
        numer(3, *whole, last_numer[:])

        logs = keep.tile([P, 4, 2, S], F32, name="logs", tag="arg3")
        rows = out.rearrange("(a t r) j -> t a r j", t=4, r=8)
        res = [keep.tile([P, S], F32, name=f"res{t}") for t in range(4)]

        def finish(t, cols):
            nc.vector.tensor_tensor(res[t][:, cols], logs[:, t, 0, cols], logs[:, t, 1, cols], ALU.subtract)
            nc.sync.dma_start(rows[t][:, :, cols], res[t][:, cols])

        nc.scalar.activation(logs[:, 0], sums[0][:], ACT.Ln)
        finish(0, whole[0])
        denom(3, halves[1], lhalves[1], sums[0][:, 0, halves[1]])
        nc.scalar.activation(logs[:, 1], sums[1][:], ACT.Ln)
        finish(1, whole[0])
        denom(3, halves[0], lhalves[0], sums[1][:, 0, halves[0]])
        nc.scalar.activation(logs[:, 2], sums[2][:], ACT.Ln)
        nc.scalar.activation(logs[:, 3, 0, :], last_numer[:], ACT.Ln)
        nc.scalar.activation(logs[:, 3, 1, halves[1]], sums[0][:, 0, halves[1]], ACT.Ln)
        nc.scalar.activation(logs[:, 3, 1, halves[0]], sums[1][:, 0, halves[0]], ACT.Ln)
        finish(2, whole[0])
        finish(3, halves[1])
        finish(3, halves[0])
